import numpy as np
import ml_dtypes


def mxq(x, axis, fmt="e4m3"):
    dtype, down = {"e4m3": (ml_dtypes.float8_e4m3fn, 7), "e5m2": (ml_dtypes.float8_e5m2, 14)}[fmt]
    v = np.moveaxis(np.asarray(x, np.float32).astype(ml_dtypes.bfloat16).astype(np.float64), axis, -1)
    blocks = v.reshape(v.shape[:-1] + (-1, 32))
    amax = np.abs(blocks).max(-1, keepdims=True)
    byte = np.maximum(np.where(amax > 0, np.frexp(amax)[1] - 1 + 127, 0) - down, 1)
    scale = np.exp2(byte - 127.0)
    codes = (blocks / scale).astype(np.float32).astype(dtype).astype(np.float64)
    return np.moveaxis((codes * scale).reshape(v.shape), -1, axis)


WIDE = False


def mx_kscale(k):
    if not WIDE:
        return np.ones(k)
    levels = np.array([10, -10, 5, -5, 0])
    if k % 512:
        return np.exp2(np.random.permutation(np.resize(levels, k // 32))).repeat(32)
    a = np.empty((k // 512, 16))
    for p in range(k // 512):
        a[p, :8] = np.random.permutation(np.resize(levels, 8))
        for g in range(8):
            far = levels[np.abs(levels - a[p, g]) >= 10]
            a[p, g + 8] = far[np.random.randint(len(far))]
    return np.exp2(a.ravel()).repeat(32)


def f64(x):
    return np.asarray(x).astype(np.float64)


def striped(idx):
    return np.tile(idx.reshape(-1, 16).T, (8, 1)).astype(np.uint16)


def unstriped(offs):
    return offs[:16].T.reshape(-1).astype(np.int64)


E2M1 = np.array([0.0, 0.5, 1.0, 1.5, 2.0, 3.0, 4.0, 6.0, -0.0, -0.5, -1.0, -1.5, -2.0, -3.0, -4.0, -6.0])


def pack_weight(w, fmt):
    k, n = w.shape
    w = f64(np.asarray(w, np.float32).astype(ml_dtypes.bfloat16)).reshape(k // 32, 32, n)
    amax = np.abs(w).max(1)
    if fmt == "e4m3":
        byte = np.frexp(amax)[1] - 1 + 127 - 7
    else:
        mant, ex = np.frexp(amax / 6.0)
        byte = np.where(mant > 0.5, ex, ex - 1) + 127
    byte = np.clip(np.where(amax > 0, byte, 1), 1, 254)
    scaled = (w * np.exp2(127.0 - byte)[:, None, :]).reshape(k, n).astype(np.float32)
    by_word = np.ascontiguousarray(scaled.reshape(k // 512, 128, 4, n).transpose(0, 1, 3, 2))
    if fmt == "e4m3":
        words = by_word.astype(ml_dtypes.float8_e4m3fn).view(np.uint8)
    else:
        c = by_word.astype(ml_dtypes.float4_e2m1fn).view(np.uint8) & 0xF
        words = (c[..., 0::2] | (c[..., 1::2] << 4)).reshape(k // 512, 128, 2 * n)
    return np.ascontiguousarray(words), np.ascontiguousarray(byte.astype(np.uint8).reshape(k // 512, 16, n))


def unpack_weight(words, scales, fmt):
    g, _, n = scales.shape
    words = np.ascontiguousarray(words).reshape(g, 128, n, -1)
    if fmt == "e4m3":
        vals = words.view(ml_dtypes.float8_e4m3fn).astype(np.float64)
    else:
        nib = np.empty((g, 128, n, 4), np.uint8)
        nib[..., 0::2] = words & 0xF
        nib[..., 1::2] = words >> 4
        vals = E2M1[nib]
    vals = vals * np.repeat(np.exp2(scales.astype(np.float64) - 127.0), 8, axis=1)[..., None]
    return vals.transpose(0, 1, 3, 2).reshape(g * 512, n)


def gelu(v):
    return 0.5 * v * (1.0 + np.tanh(np.sqrt(2.0 / np.pi) * (v + 0.044715 * v**3)))


K, KB, H, T, S, P = 1536, 1024, 1024, 4096, 1024, 512

def setup_inputs():
    n = np.random.standard_normal
    s = mx_kscale(K)[:, None]
    u = mx_kscale(H)
    tab_words, tab_scales = pack_weight(n((K, T)) * s, "e4m3")
    w4_words, w4_scales = pack_weight(n((KB, H)) * 1.5 / np.sqrt(K) / s[:KB], "e2m1")
    w1 = n((K - KB, H)) * 1.5 / np.sqrt(K) / s[KB:]
    return {
        "tab_words": tab_words, "tab_scales": tab_scales,
        "offs": striped(np.random.permutation(T)[:S]),
        "pos1": striped(np.random.permutation(S)[:P]),
        "pos2": striped(np.random.permutation(S)[:P]),
        "w4_words": w4_words, "w4_scales": w4_scales,
        "w1": w1.astype(np.float32),
        "gain": (np.exp(0.2 * n(H)) * u).astype(np.float32),
        "shift": (0.3 * n(H) * u).astype(np.float32),
        "focus": (0.9 * np.random.uniform(0.5, 1.5, H) / np.sqrt(H) / u ** 2).astype(np.float32),
        "sway": np.random.uniform(1.0, 3.0, P).astype(np.float32),
    }

def reference(tab_words, tab_scales, offs, pos1, pos2, w4_words, w4_scales, w1, gain, shift, focus, sway):
    v = unpack_weight(tab_words, tab_scales, "e4m3")[:, unstriped(offs)]
    w4 = unpack_weight(w4_words, w4_scales, "e2m1")
    w1q = mxq(f64(w1), 0, "e4m3")
    a = w4.T @ v[:KB] + w1q.T @ v[KB:]
    h = np.tanh(a) * f64(gain)[:, None] + f64(shift)[:, None]
    x1 = h[:, unstriped(pos1)]
    x2 = np.abs(h[:, unstriped(pos2)]) * f64(focus)[:, None]
    e = mxq(x1, 0, "e4m3").T @ mxq(x2, 0, "e4m3")
    return e + np.sin(e) * f64(sway)[None, :]

@@ -1,0 +1,255 @@
+import math
+from contextlib import ExitStack
+
+import concourse.mybir as mybir
+
+F32 = mybir.dt.float32
+BF16 = mybir.dt.bfloat16
+I32 = mybir.dt.int32
+U32 = mybir.dt.uint32
+U16 = mybir.dt.uint16
+U8 = mybir.dt.uint8
+FP8X4 = mybir.dt.float8_e4m3fn_x4
+FP4X4 = mybir.dt.float4_e2m1fn_x4
+ALU = mybir.AluOpType
+ACT = mybir.ActivationFunctionType
+
+K, KB, H, T, S, P = 1536, 1024, 1024, 4096, 1024, 512
+FLOPS = 2 * K * H * S + 2 * H * P * P
+NP = 128
+HALF = 256
+
+
+def tile_list_setter_tempo_fit_kernel(
+    tc, tab_words, tab_scales, offs, pos1, pos2, w4_words, w4_scales, w1, gain, shift, focus, sway, out
+):
+    nc = tc.nc
+    with ExitStack() as ctx:
+        lists = ctx.enter_context(tc.tile_pool(name="lists", bufs=1))
+        sb = ctx.enter_context(tc.tile_pool(name="sb", bufs=1))
+        ep = ctx.enter_context(tc.tile_pool(name="ep", bufs=2))
+        ps = ctx.enter_context(tc.psum_pool(name="ps", bufs=1))
+
+        offs_t = lists.tile([NP, S // 16], U16, name="offs_t")
+        pos1_t = lists.tile([NP, P // 16], U16, name="pos1_t")
+        pos2_t = lists.tile([NP, P // 16], U16, name="pos2_t")
+
+        tab = [sb.tile([NP, T], I32, name="tab%d" % a, tag="tab%d" % a, align_bytes=64) for a in range(3)]
+        win = sb.tile([NP, T], U8, name="win", tag="win", align_bytes=64)
+        wsr = sb.tile([NP, 2, H], U8, name="wsr")
+        ms = [sb.tile([NP, S], U8, name="ms%d" % a, align_bytes=64) for a in range(2)]
+        w4r = sb.tile([NP, 2, H // 2], I32, name="w4r")
+        w1r = [sb.tile([NP, 4, 512], F32, name="w1r%d" % b) for b in range(2)]
+        rows = sb.tile([NP, 2, 128], F32, name="rows")
+        dealt = sb.tile([NP, 256], F32, name="dealt", align_bytes=64)
+        turned = sb.tile([NP, 8, 32], F32, name="turned", align_bytes=64)
+        sway_t = sb.tile([NP, P], F32, name="sway_t")
+
+        def load_tab(a):
+            nc.sync.dma_start(out=tab[a][:], in_=tab_words[a].rearrange("p t i -> p (t i)").bitcast(I32))
+
+        def load_w1(b):
+            nc.sync.dma_start(
+                out=w1r[b][:], in_=w1[:, 512 * b : 512 * (b + 1)].rearrange("(p j) w -> p j w", j=4)
+            )
+
+        nc.gpsimd.memset(win[:].bitcast(I32), 0)
+        for a in range(2):
+            nc.vector.memset(ms[a][:].bitcast(I32), 0)
+
+        def load_rows(v, src):
+            nc.sync.dma_start(out=rows[v:NP:32], in_=src.rearrange("(b g n) -> g b n", b=2, g=4))
+
+        load_tab(0)
+        nc.sync.dma_start(out=w4r[:], in_=w4_words.rearrange("a p n -> p a n").bitcast(I32))
+        for q in range(4):
+            nc.sync.dma_start(
+                out=wsr[32 * q : 32 * q + 4, :, :].bitcast(I32),
+                in_=w4_scales[:, 4 * q : 4 * q + 4, :].rearrange("a r n -> r a n").bitcast(I32),
+            )
+        nc.sync.dma_start(offs_t[:], offs)
+        load_w1(0)
+        load_rows(0, gain)
+        load_tab(1)
+        load_rows(1, shift)
+        load_rows(2, focus)
+        load_tab(2)
+        nc.sync.dma_start(pos2_t[:], pos2)
+        nc.sync.dma_start(pos1_t[:], pos1)
+        load_w1(1)
+        nc.sync.dma_start(out=sway_t[:], in_=sway.partition_broadcast(NP))
+
+        for q in range(4):
+            nc.gpsimd.dma_start(
+                out=win[32 * q + 4 : 32 * q + 16, :].bitcast(I32),
+                in_=tab_scales[:, 4 * q : 4 * q + 4, :].bitcast(I32),
+            )
+
+        gs = sb.tile([NP, S], U8, name="gs", align_bytes=64)
+        nc.vector.tensor_copy(gs[:], win[:].indirect(offs_t[:]))
+        for a in range(2):
+            r0 = 4 + 4 * a
+            nc.gpsimd.dma_start(out=ms[a][0:100, :].bitcast(I32), in_=gs[r0 : r0 + 100, :].bitcast(I32))
+        gw = [sb.tile([NP, S], U32, name="gw%d" % a, tag=("win", "gw1")[a], align_bytes=64) for a in range(2)]
+        gw2 = [sb.tile([NP, 512], U32, name="gw2%d" % h, align_bytes=64) for h in range(2)]
+        nc.vector.tensor_copy(gw[0][:], tab[0][:].bitcast(U32).indirect(offs_t[:]))
+
+        w4p = sb.tile([NP, 2, 8, 256], U8, name="w4p", align_bytes=64)
+        wsp = sb.tile([NP, 2, 8, 128], U8, name="wsp", align_bytes=64)
+        nc.vector.tensor_copy(
+            out=w4p[:].rearrange("p a c n -> p (a c n)").bitcast(I32).rearrange("p (g t q w) -> p g t q w", g=4, t=4, w=4),
+            in_=w4r[:].rearrange("p a (b q t w) -> p (a b) t q w", b=2, t=4, w=4),
+        )
+        wsp_words = wsp[:].rearrange("p a c n -> p (a c n)").bitcast(I32)
+        wsr_words = wsr[:].rearrange("p a n -> p (a n)").bitcast(I32)
+        nc.vector.memset(wsp_words, 0)
+        for q in range(4):
+            live = slice(32 * q, 32 * q + 4)
+            nc.vector.tensor_copy(
+                out=wsp_words[live].rearrange("p (g t q w) -> p g t q w", g=4, t=4, w=2),
+                in_=wsr_words[live].rearrange("p (g q t w) -> p g t q w", g=4, t=4, w=2),
+            )
+
+        w1b = [sb.tile([NP, 2048], BF16, name="w1b%d" % b, tag=("w1b", "tab2")[b], align_bytes=64) for b in range(2)]
+        w1c = [sb.tile([NP, 512], U32, name="w1c%d" % b, align_bytes=64) for b in range(2)]
+        w1s = [sb.tile([NP, 512], U8, name="w1s%d" % b, align_bytes=64) for b in range(2)]
+
+        def round_w1(b, copy):
+            copy(
+                out=w1b[b][:].rearrange("p (t q i j) -> p t q i j", t=4, i=8, j=4),
+                in_=w1r[b][:].rearrange("p j (q t i) -> p t q i j", t=4, i=8),
+            )
+            nc.vector.quantize_mx(out=w1c[b][:].bitcast(FP8X4), scales=w1s[b][:], in_=w1b[b][:])
+
+        round_w1(0, nc.scalar.copy)
+        nc.vector.tensor_copy(gw[1][:], tab[1][:].bitcast(U32).indirect(offs_t[:]))
+        nc.vector.memset(dealt[:], 0.0)
+        for g in range(4):
+            live = slice(32 * g, 32 * g + 3)
+            nc.vector.tensor_copy(
+                out=dealt[live].rearrange("p (b t r i) -> p b t r i", b=2, t=4, i=8),
+                in_=rows[live].rearrange("p b (r t i) -> p b t r i", t=4, i=8),
+            )
+        nc.vector.transpose(turned[:].rearrange("p c v -> p (c v)"), dealt[:])
+        sgn = sb.tile([NP, 8], F32, name="sgn")
+        fac = [sb.tile([NP, 8], F32, name="fac%d" % v) for v in range(4)]
+        nc.vector.tensor_scalar(sgn[:], turned[:, :, 2], 0.0, 2.0, ALU.is_ge, ALU.mult)
+        for v in range(2):
+            nc.vector.scalar_tensor_tensor(fac[v][:], sgn[:], -1.0, turned[:, :, v], ALU.add, ALU.mult)
+            nc.vector.tensor_tensor(fac[2 + v][:], turned[:, :, v], turned[:, :, 2], ALU.mult)
+
+        for h in range(2):
+            nc.vector.tensor_copy(gw2[h][:], tab[2][:].bitcast(U32).indirect(offs_t[:, 32 * h : 32 * (h + 1)]))
+        round_w1(1, nc.vector.tensor_copy)
+
+        tanh_t = [sb.tile([NP, S], F32, name="tanh%d" % c) for c in range(8)]
+
+        def first_pass(acc, c, h, a):
+            cols = slice(512 * h, 512 * (h + 1))
+            if a < 2:
+                nc.tensor.matmul_mx(
+                    out=acc[:],
+                    lhsT=w4p[:, a, c, :].bitcast(FP4X4),
+                    lhsT_scale=wsp[:, a, c, :],
+                    rhs=gw[a][:, cols].bitcast(FP8X4),
+                    rhs_scale=ms[a][:, cols],
+                    start=(a == 0),
+                    stop=False,
+                )
+            else:
+                b, t = divmod(c, 4)
+                wc = slice(128 * t, 128 * (t + 1))
+                nc.tensor.matmul_mx(
+                    out=acc[:],
+                    lhsT=w1c[b][:, wc].bitcast(FP8X4),
+                    lhsT_scale=w1s[b][:, wc],
+                    rhs=gw2[h][:].bitcast(FP8X4),
+                    rhs_scale=gs[12:NP, cols],
+                    start=False,
+                    stop=True,
+                )
+                nc.scalar.activation(tanh_t[c][:, cols], acc[:], ACT.Tanh)
+
+        early = [[ps.tile([NP, 512], F32, name="acc%d_%d" % (c, h), tag="bank%d" % (2 * c + h)) for h in range(2)] for c in range(4)]
+        for a in range(3):
+            for c in range(4):
+                for h in range(2):
+                    first_pass(early[c][h], c, h, a)
+        for c in range(4, 8):
+            for h in range(2):
+                acc = ps.tile([NP, 512], F32, name="acc%d_%d" % (c, h), tag="bank%d" % (2 * (c % 2) + h))
+                for a in range(3):
+                    first_pass(acc, c, h, a)
+
+        ring = sb.tile([NP, 5 * 768], F32, name="ring")
+        pl2 = [sb.tile([NP, 4, P], BF16, name="pl2_%d" % b) for b in range(2)]
+        pl1 = [[sb.tile([NP, 4, HALF], BF16, name="pl1_%d_%d" % (u, b)) for b in range(2)] for u in range(2)]
+        il2 = [sb.tile([NP, P, 4], BF16, name="il2_%d" % b, align_bytes=64) for b in range(2)]
+        il1 = [[sb.tile([NP, HALF, 4], BF16, name="il1_%d_%d" % (u, b), align_bytes=64) for b in range(2)] for u in range(2)]
+        c2 = [sb.tile([NP, P], U32, name="c2_%d" % b, align_bytes=64) for b in range(2)]
+        s2 = [sb.tile([NP, P], U8, name="s2_%d" % b, align_bytes=64) for b in range(2)]
+        c1 = [[sb.tile([NP, HALF], U32, name="c1_%d_%d" % (u, b), align_bytes=64) for b in range(2)] for u in range(2)]
+        s1 = [[sb.tile([NP, HALF], U8, name="s1_%d_%d" % (u, b), align_bytes=64) for b in range(2)] for u in range(2)]
+        e_ps = [ps.tile([NP, P], F32, name="e%d" % m, tag="bank%d" % (4 + m)) for m in range(4)]
+
+        def pick2(c, at):
+            b, t = divmod(c, 4)
+            g = ring[:, at : at + P]
+            nc.vector.tensor_copy(g, tanh_t[c][:].indirect(pos2_t[:]))
+            nc.scalar.activation(pl2[b][:, t, :], g, ACT.Abs, bias=fac[3][:, c : c + 1], scale=fac[2][:, c : c + 1])
+
+        def pick1(u, c, at):
+            b, t = divmod(c, 4)
+            g = ring[:, at : at + HALF]
+            nc.vector.tensor_copy(g, tanh_t[c][:].indirect(pos1_t[:, 16 * u : 16 * (u + 1)]))
+            nc.scalar.activation(pl1[u][b][:, t, :], g, ACT.Identity, bias=fac[1][:, c : c + 1], scale=fac[0][:, c : c + 1])
+
+        def weave(copy, dst, src, codes, scales):
+            copy(
+                out=dst[:].rearrange("p (c i) t -> p c t i", i=4),
+                in_=src[:].rearrange("p t (c i) -> p c t i", i=4),
+            )
+            nc.vector.quantize_mx(out=codes[:].bitcast(FP8X4), scales=scales[:], in_=dst[:].rearrange("p n t -> p (n t)"))
+
+        def second_pass(u, b):
+            for mm in range(2):
+                mc = slice(128 * mm, 128 * (mm + 1))
+                nc.tensor.matmul_mx(
+                    out=e_ps[2 * u + mm][:],
+                    lhsT=c1[u][b][:, mc].bitcast(FP8X4),
+                    lhsT_scale=s1[u][b][:, mc],
+                    rhs=c2[b][:].bitcast(FP8X4),
+                    rhs_scale=s2[b][:],
+                    start=(b == 0),
+                    stop=(b == 1),
+                )
+
+        def finish(m):
+            turns = ep.tile([NP, P], I32, name="turns")
+            frac = ep.tile([NP, P], F32, name="frac")
+            wave = ep.tile([NP, P], F32, name="wave")
+            res = sb.tile([NP, P], F32, name="res%d" % m)
+            nc.vector.tensor_scalar(turns[:], e_ps[m][:], 1.0 / (2.0 * math.pi), None, ALU.mult)
+            nc.vector.scalar_tensor_tensor(frac[:], e_ps[m][:], 1.0 / (2.0 * math.pi), turns[:], ALU.mult, ALU.subtract)
+            nc.scalar.activation(wave[:], frac[:], ACT.Sin, scale=2.0 * math.pi)
+            nc.vector.tensor_tensor(frac[:], wave[:], sway_t[:], ALU.mult)
+            nc.vector.tensor_tensor(res[:], e_ps[m][:], frac[:], ALU.add)
+            nc.sync.dma_start(out=out[128 * m : 128 * (m + 1), :], in_=res[:])
+
+        for c in range(8):
+            at = 768 * (c % 5)
+            pick2(c, at)
+            pick1(0, c, at + P)
+            if c % 4 == 3:
+                b = c // 4
+                weave(nc.scalar.copy, il2[b], pl2[b], c2[b], s2[b])
+                weave(nc.scalar.copy, il1[0][b], pl1[0][b], c1[0][b], s1[0][b])
+                second_pass(0, b)
+        for c in range(8):
+            pick1(1, c, 768 + HALF * (c % 6))
+            if c % 4 == 3:
+                b = c // 4
+                weave(nc.scalar.copy, il1[1][b], pl1[1][b], c1[1][b], s1[1][b])
+                second_pass(1, b)
+        for m in range(4):
+            finish(m)

@@ -27,23 +27,24 @@ def tile_list_setter_tempo_fit_kernel(
     with ExitStack() as ctx:
         lists = ctx.enter_context(tc.tile_pool(name="lists", bufs=1))
         sb = ctx.enter_context(tc.tile_pool(name="sb", bufs=1))
-        ep = ctx.enter_context(tc.tile_pool(name="ep", bufs=2))
+        ep = ctx.enter_context(tc.tile_pool(name="ep", bufs=3))
         ps = ctx.enter_context(tc.psum_pool(name="ps", bufs=1))
 
         offs_t = lists.tile([NP, S // 16], U16, name="offs_t")
         pos1_t = lists.tile([NP, P // 16], U16, name="pos1_t")
         pos2_t = lists.tile([NP, P // 16], U16, name="pos2_t")
 
-        tab = [sb.tile([NP, T], I32, name="tab%d" % a, tag="tab%d" % a, align_bytes=64) for a in range(3)]
+        tab = [sb.tile([NP, T], I32, name="tab%d" % a, tag=("tab0", "tab1", "win")[a], align_bytes=64) for a in range(3)]
         win = sb.tile([NP, T], U8, name="win", tag="win", align_bytes=64)
         wsr = sb.tile([NP, 2, H], U8, name="wsr")
-        ms = [sb.tile([NP, S], U8, name="ms%d" % a, align_bytes=64) for a in range(2)]
+        ms = sb.tile([NP, S], U8, name="ms", align_bytes=64)
+        stage = sb.tile([NP, T // 4], I32, name="stage")
         w4r = sb.tile([NP, 2, H // 2], I32, name="w4r")
-        w1r = [sb.tile([NP, 4, 512], F32, name="w1r%d" % b) for b in range(2)]
+        w1r = [sb.tile([NP, 4, 512], F32, name="w1r%d" % b, tag="w1r", align_bytes=64) for b in range(2)]
         rows = sb.tile([NP, 2, 128], F32, name="rows")
         dealt = sb.tile([NP, 256], F32, name="dealt", align_bytes=64)
         turned = sb.tile([NP, 8, 32], F32, name="turned", align_bytes=64)
-        sway_t = sb.tile([NP, P], F32, name="sway_t")
+        sway_t = sb.tile([NP, P], F32, name="sway_t", tag="tab1", align_bytes=64)
 
         def load_tab(a):
             nc.sync.dma_start(out=tab[a][:], in_=tab_words[a].rearrange("p t i -> p (t i)").bitcast(I32))
@@ -53,44 +54,40 @@ def tile_list_setter_tempo_fit_kernel(
                 out=w1r[b][:], in_=w1[:, 512 * b : 512 * (b + 1)].rearrange("(p j) w -> p j w", j=4)
             )
 
-        nc.gpsimd.memset(win[:].bitcast(I32), 0)
-        for a in range(2):
-            nc.vector.memset(ms[a][:].bitcast(I32), 0)
+        nc.vector.memset(win[:].bitcast(I32), 0)
+        nc.vector.memset(ms[:].bitcast(I32), 0)
 
         def load_rows(v, src):
-            nc.sync.dma_start(out=rows[v:NP:32], in_=src.rearrange("(b g n) -> g b n", b=2, g=4))
+            nc.gpsimd.dma_start(out=rows[v:NP:32], in_=src.rearrange("(b g n) -> g b n", b=2, g=4))
 
+        for q in range(4):
+            nc.scalar.dma_start(
+                out=stage[32 * q : 32 * q + 12, :],
+                in_=tab_scales[:, 4 * q : 4 * q + 4, :].bitcast(I32),
+            )
+        nc.sync.dma_start(offs_t[:], offs)
         load_tab(0)
-        nc.sync.dma_start(out=w4r[:], in_=w4_words.rearrange("a p n -> p a n").bitcast(I32))
         for q in range(4):
             nc.sync.dma_start(
                 out=wsr[32 * q : 32 * q + 4, :, :].bitcast(I32),
                 in_=w4_scales[:, 4 * q : 4 * q + 4, :].rearrange("a r n -> r a n").bitcast(I32),
             )
-        nc.sync.dma_start(offs_t[:], offs)
+        nc.sync.dma_start(out=w4r[:], in_=w4_words.rearrange("a p n -> p a n").bitcast(I32))
         load_w1(0)
-        load_rows(0, gain)
         load_tab(1)
-        load_rows(1, shift)
-        load_rows(2, focus)
-        load_tab(2)
         nc.sync.dma_start(pos2_t[:], pos2)
         nc.sync.dma_start(pos1_t[:], pos1)
-        load_w1(1)
-        nc.sync.dma_start(out=sway_t[:], in_=sway.partition_broadcast(NP))
+        for v, src in enumerate((gain, shift, focus)):
+            load_rows(v, src)
 
         for q in range(4):
-            nc.gpsimd.dma_start(
-                out=win[32 * q + 4 : 32 * q + 16, :].bitcast(I32),
-                in_=tab_scales[:, 4 * q : 4 * q + 4, :].bitcast(I32),
-            )
-
+            live = slice(32 * q, 32 * q + 12)
+            nc.vector.tensor_copy(out=win[:].bitcast(I32)[live], in_=stage[live])
         gs = sb.tile([NP, S], U8, name="gs", align_bytes=64)
         nc.vector.tensor_copy(gs[:], win[:].indirect(offs_t[:]))
-        for a in range(2):
-            r0 = 4 + 4 * a
-            nc.gpsimd.dma_start(out=ms[a][0:100, :].bitcast(I32), in_=gs[r0 : r0 + 100, :].bitcast(I32))
-        gw = [sb.tile([NP, S], U32, name="gw%d" % a, tag=("win", "gw1")[a], align_bytes=64) for a in range(2)]
+        nc.sync.dma_start(out=ms[0:112, :].bitcast(I32), in_=gs[4:116, :].bitcast(I32))
+        load_tab(2)
+        gw = [sb.tile([NP, S], U32, name="gw%d" % a, tag=("gw0", "gw1")[a], align_bytes=64) for a in range(2)]
         gw2 = [sb.tile([NP, 512], U32, name="gw2%d" % h, align_bytes=64) for h in range(2)]
         nc.vector.tensor_copy(gw[0][:], tab[0][:].bitcast(U32).indirect(offs_t[:]))
 
@@ -110,7 +107,7 @@ def tile_list_setter_tempo_fit_kernel(
                 in_=wsr_words[live].rearrange("p (g q t w) -> p g t q w", g=4, t=4, w=2),
             )
 
-        w1b = [sb.tile([NP, 2048], BF16, name="w1b%d" % b, tag=("w1b", "tab2")[b], align_bytes=64) for b in range(2)]
+        w1b = [sb.tile([NP, 2048], BF16, name="w1b%d" % b, tag=("w1b", "win")[b], align_bytes=64) for b in range(2)]
         w1c = [sb.tile([NP, 512], U32, name="w1c%d" % b, align_bytes=64) for b in range(2)]
         w1s = [sb.tile([NP, 512], U8, name="w1s%d" % b, align_bytes=64) for b in range(2)]
 
@@ -122,7 +119,9 @@ def tile_list_setter_tempo_fit_kernel(
             nc.vector.quantize_mx(out=w1c[b][:].bitcast(FP8X4), scales=w1s[b][:], in_=w1b[b][:])
 
         round_w1(0, nc.scalar.copy)
+        load_w1(1)
         nc.vector.tensor_copy(gw[1][:], tab[1][:].bitcast(U32).indirect(offs_t[:]))
+        nc.sync.dma_start(out=sway_t[:], in_=sway.partition_broadcast(NP))
         nc.vector.memset(dealt[:], 0.0)
         for g in range(4):
             live = slice(32 * g, 32 * g + 3)
@@ -152,7 +151,7 @@ def tile_list_setter_tempo_fit_kernel(
                     lhsT=w4p[:, a, c, :].bitcast(FP4X4),
                     lhsT_scale=wsp[:, a, c, :],
                     rhs=gw[a][:, cols].bitcast(FP8X4),
-                    rhs_scale=ms[a][:, cols],
+                    rhs_scale=(gs, ms)[a][:, cols],
                     start=(a == 0),
                     stop=False,
                 )
@@ -164,7 +163,7 @@ def tile_list_setter_tempo_fit_kernel(
                     lhsT=w1c[b][:, wc].bitcast(FP8X4),
                     lhsT_scale=w1s[b][:, wc],
                     rhs=gw2[h][:].bitcast(FP8X4),
-                    rhs_scale=gs[12:NP, cols],
+                    rhs_scale=gs[8:NP, cols],
                     start=False,
                     stop=True,
                 )
@@ -181,7 +180,7 @@ def tile_list_setter_tempo_fit_kernel(
                 for a in range(3):
                     first_pass(acc, c, h, a)
 
-        ring = sb.tile([NP, 5 * 768], F32, name="ring")
+        ring = sb.tile([NP, 5 * 768 + 8 * HALF], F32, name="ring")
         pl2 = [sb.tile([NP, 4, P], BF16, name="pl2_%d" % b) for b in range(2)]
         pl1 = [[sb.tile([NP, 4, HALF], BF16, name="pl1_%d_%d" % (u, b)) for b in range(2)] for u in range(2)]
         il2 = [sb.tile([NP, P, 4], BF16, name="il2_%d" % b, align_bytes=64) for b in range(2)]
@@ -202,7 +201,7 @@ def tile_list_setter_tempo_fit_kernel(
             b, t = divmod(c, 4)
             g = ring[:, at : at + HALF]
             nc.vector.tensor_copy(g, tanh_t[c][:].indirect(pos1_t[:, 16 * u : 16 * (u + 1)]))
-            nc.scalar.activation(pl1[u][b][:, t, :], g, ACT.Identity, bias=fac[1][:, c : c + 1], scale=fac[0][:, c : c + 1])
+            nc.gpsimd.tensor_scalar(pl1[u][b][:, t, :], g, fac[0][:, c : c + 1], fac[1][:, c : c + 1], ALU.mult, ALU.add)
 
         def weave(copy, dst, src, codes, scales):
             copy(
@@ -232,7 +231,7 @@ def tile_list_setter_tempo_fit_kernel(
             nc.vector.tensor_scalar(turns[:], e_ps[m][:], 1.0 / (2.0 * math.pi), None, ALU.mult)
             nc.vector.scalar_tensor_tensor(frac[:], e_ps[m][:], 1.0 / (2.0 * math.pi), turns[:], ALU.mult, ALU.subtract)
             nc.scalar.activation(wave[:], frac[:], ACT.Sin, scale=2.0 * math.pi)
-            nc.vector.tensor_tensor(frac[:], wave[:], sway_t[:], ALU.mult)
+            (nc.gpsimd, nc.vector)[m // 2].tensor_tensor(frac[:], wave[:], sway_t[:], ALU.mult)
             nc.vector.tensor_tensor(res[:], e_ps[m][:], frac[:], ALU.add)
             nc.sync.dma_start(out=out[128 * m : 128 * (m + 1), :], in_=res[:])
 
@@ -242,11 +241,11 @@ def tile_list_setter_tempo_fit_kernel(
             pick1(0, c, at + P)
             if c % 4 == 3:
                 b = c // 4
-                weave(nc.scalar.copy, il2[b], pl2[b], c2[b], s2[b])
+                weave((nc.scalar.copy, nc.vector.tensor_copy)[b], il2[b], pl2[b], c2[b], s2[b])
                 weave(nc.scalar.copy, il1[0][b], pl1[0][b], c1[0][b], s1[0][b])
                 second_pass(0, b)
         for c in range(8):
-            pick1(1, c, 768 + HALF * (c % 6))
+            pick1(1, c, 5 * 768 + HALF * c)
             if c % 4 == 3:
                 b = c // 4
                 weave(nc.scalar.copy, il1[1][b], pl1[1][b], c1[1][b], s1[1][b])

@@ -27,7 +27,7 @@ def tile_list_setter_tempo_fit_kernel(
     with ExitStack() as ctx:
         lists = ctx.enter_context(tc.tile_pool(name="lists", bufs=1))
         sb = ctx.enter_context(tc.tile_pool(name="sb", bufs=1))
-        ep = ctx.enter_context(tc.tile_pool(name="ep", bufs=3))
+        ep = ctx.enter_context(tc.tile_pool(name="ep", bufs=4))
         ps = ctx.enter_context(tc.psum_pool(name="ps", bufs=1))
 
         offs_t = lists.tile([NP, S // 16], U16, name="offs_t")
@@ -56,6 +56,7 @@ def tile_list_setter_tempo_fit_kernel(
 
         nc.vector.memset(win[:].bitcast(I32), 0)
         nc.vector.memset(ms[:].bitcast(I32), 0)
+        nc.vector.memset(dealt[:], 0.0)
 
         def load_rows(v, src):
             nc.gpsimd.dma_start(out=rows[v:NP:32], in_=src.rearrange("(b g n) -> g b n", b=2, g=4))
@@ -65,6 +66,8 @@ def tile_list_setter_tempo_fit_kernel(
                 out=stage[32 * q : 32 * q + 12, :],
                 in_=tab_scales[:, 4 * q : 4 * q + 4, :].bitcast(I32),
             )
+        warm = sb.tile([NP, 1], F32, name="warm")
+        nc.scalar.activation(warm[:], dealt[:, 0:1], ACT.Silu)
         nc.sync.dma_start(offs_t[:], offs)
         load_tab(0)
         for q in range(4):
@@ -122,7 +125,6 @@ def tile_list_setter_tempo_fit_kernel(
         load_w1(1)
         nc.vector.tensor_copy(gw[1][:], tab[1][:].bitcast(U32).indirect(offs_t[:]))
         nc.sync.dma_start(out=sway_t[:], in_=sway.partition_broadcast(NP))
-        nc.vector.memset(dealt[:], 0.0)
         for g in range(4):
             live = slice(32 * g, 32 * g + 3)
             nc.vector.tensor_copy(
@@ -180,9 +182,10 @@ def tile_list_setter_tempo_fit_kernel(
                 for a in range(3):
                     first_pass(acc, c, h, a)
 
-        ring = sb.tile([NP, 5 * 768 + 8 * HALF], F32, name="ring")
+        ring = sb.tile([NP, 5 * P], F32, name="ring")
+        picked1 = [sb.tile([NP, P], F32, name="picked1_%d" % c) for c in range(3)]
         pl2 = [sb.tile([NP, 4, P], BF16, name="pl2_%d" % b) for b in range(2)]
-        pl1 = [[sb.tile([NP, 4, HALF], BF16, name="pl1_%d_%d" % (u, b)) for b in range(2)] for u in range(2)]
+        pl1 = [sb.tile([NP, 4, P], BF16, name="pl1_%d" % b) for b in range(2)]
         il2 = [sb.tile([NP, P, 4], BF16, name="il2_%d" % b, align_bytes=64) for b in range(2)]
         il1 = [[sb.tile([NP, HALF, 4], BF16, name="il1_%d_%d" % (u, b), align_bytes=64) for b in range(2)] for u in range(2)]
         c2 = [sb.tile([NP, P], U32, name="c2_%d" % b, align_bytes=64) for b in range(2)]
@@ -197,16 +200,16 @@ def tile_list_setter_tempo_fit_kernel(
             nc.vector.tensor_copy(g, tanh_t[c][:].indirect(pos2_t[:]))
             nc.scalar.activation(pl2[b][:, t, :], g, ACT.Abs, bias=fac[3][:, c : c + 1], scale=fac[2][:, c : c + 1])
 
-        def pick1(u, c, at):
+        def pick1(c):
             b, t = divmod(c, 4)
-            g = ring[:, at : at + HALF]
-            nc.vector.tensor_copy(g, tanh_t[c][:].indirect(pos1_t[:, 16 * u : 16 * (u + 1)]))
-            nc.gpsimd.tensor_scalar(pl1[u][b][:, t, :], g, fac[0][:, c : c + 1], fac[1][:, c : c + 1], ALU.mult, ALU.add)
+            g = picked1[c % 3][:]
+            nc.vector.tensor_copy(g, tanh_t[c][:].indirect(pos1_t[:]))
+            nc.gpsimd.tensor_scalar(pl1[b][:, t, :], g, fac[0][:, c : c + 1], fac[1][:, c : c + 1], ALU.mult, ALU.add)
 
         def weave(copy, dst, src, codes, scales):
             copy(
                 out=dst[:].rearrange("p (c i) t -> p c t i", i=4),
-                in_=src[:].rearrange("p t (c i) -> p c t i", i=4),
+                in_=src.rearrange("p t (c i) -> p c t i", i=4),
             )
             nc.vector.quantize_mx(out=codes[:].bitcast(FP8X4), scales=scales[:], in_=dst[:].rearrange("p n t -> p (n t)"))
 
@@ -231,24 +234,18 @@ def tile_list_setter_tempo_fit_kernel(
             nc.vector.tensor_scalar(turns[:], e_ps[m][:], 1.0 / (2.0 * math.pi), None, ALU.mult)
             nc.vector.scalar_tensor_tensor(frac[:], e_ps[m][:], 1.0 / (2.0 * math.pi), turns[:], ALU.mult, ALU.subtract)
             nc.scalar.activation(wave[:], frac[:], ACT.Sin, scale=2.0 * math.pi)
-            (nc.gpsimd, nc.vector)[m // 2].tensor_tensor(frac[:], wave[:], sway_t[:], ALU.mult)
+            (nc.gpsimd, nc.vector)[m // 3].tensor_tensor(frac[:], wave[:], sway_t[:], ALU.mult)
             nc.vector.tensor_tensor(res[:], e_ps[m][:], frac[:], ALU.add)
             nc.sync.dma_start(out=out[128 * m : 128 * (m + 1), :], in_=res[:])
 
         for c in range(8):
-            at = 768 * (c % 5)
-            pick2(c, at)
-            pick1(0, c, at + P)
+            pick2(c, P * (c % 5))
+            pick1(c)
             if c % 4 == 3:
                 b = c // 4
-                weave((nc.scalar.copy, nc.vector.tensor_copy)[b], il2[b], pl2[b], c2[b], s2[b])
-                weave(nc.scalar.copy, il1[0][b], pl1[0][b], c1[0][b], s1[0][b])
-                second_pass(0, b)
-        for c in range(8):
-            pick1(1, c, 5 * 768 + HALF * c)
-            if c % 4 == 3:
-                b = c // 4
-                weave(nc.scalar.copy, il1[1][b], pl1[1][b], c1[1][b], s1[1][b])
-                second_pass(1, b)
+                weave((nc.scalar.copy, nc.vector.tensor_copy)[b], il2[b], pl2[b][:], c2[b], s2[b])
+                for u in range(2):
+                    weave(nc.scalar.copy, il1[u][b], pl1[b][:, :, HALF * u : HALF * (u + 1)], c1[u][b], s1[u][b])
+                    second_pass(u, b)
         for m in range(4):
             finish(m)

import math
from contextlib import ExitStack

import concourse.mybir as mybir

F32 = mybir.dt.float32
BF16 = mybir.dt.bfloat16
I32 = mybir.dt.int32
U32 = mybir.dt.uint32
U16 = mybir.dt.uint16
U8 = mybir.dt.uint8
FP8X4 = mybir.dt.float8_e4m3fn_x4
FP4X4 = mybir.dt.float4_e2m1fn_x4
ALU = mybir.AluOpType
ACT = mybir.ActivationFunctionType

K, KB, H, T, S, P = 1536, 1024, 1024, 4096, 1024, 512
FLOPS = 2 * K * H * S + 2 * H * P * P
NP = 128
HALF = 256


def tile_list_setter_tempo_fit_kernel(
    tc, tab_words, tab_scales, offs, pos1, pos2, w4_words, w4_scales, w1, gain, shift, focus, sway, out
):
    nc = tc.nc
    with ExitStack() as ctx:
        lists = ctx.enter_context(tc.tile_pool(name="lists", bufs=1))
        sb = ctx.enter_context(tc.tile_pool(name="sb", bufs=1))
        ep = ctx.enter_context(tc.tile_pool(name="ep", bufs=4))
        ps = ctx.enter_context(tc.psum_pool(name="ps", bufs=1))

        offs_t = lists.tile([NP, S // 16], U16, name="offs_t")
        pos1_t = lists.tile([NP, P // 16], U16, name="pos1_t")
        pos2_t = lists.tile([NP, P // 16], U16, name="pos2_t")

        tab = [sb.tile([NP, T], I32, name="tab%d" % a, tag=("tab0", "tab1", "win")[a], align_bytes=64) for a in range(3)]
        win = sb.tile([NP, T], U8, name="win", tag="win", align_bytes=64)
        wsr = sb.tile([NP, 2, H], U8, name="wsr")
        ms = sb.tile([NP, S], U8, name="ms", align_bytes=64)
        stage = sb.tile([NP, T // 4], I32, name="stage")
        w4r = sb.tile([NP, 2, H // 2], I32, name="w4r")
        w1r = [sb.tile([NP, 4, 512], F32, name="w1r%d" % b, tag="w1r", align_bytes=64) for b in range(2)]
        rows = sb.tile([NP, 2, 128], F32, name="rows")
        dealt = sb.tile([NP, 256], F32, name="dealt", align_bytes=64)
        turned = sb.tile([NP, 8, 32], F32, name="turned", align_bytes=64)
        sway_t = sb.tile([NP, P], F32, name="sway_t", tag="tab1", align_bytes=64)

        def load_tab(a):
            nc.sync.dma_start(out=tab[a][:], in_=tab_words[a].rearrange("p t i -> p (t i)").bitcast(I32))

        def load_w1(b):
            nc.sync.dma_start(
                out=w1r[b][:], in_=w1[:, 512 * b : 512 * (b + 1)].rearrange("(p j) w -> p j w", j=4)
            )

        nc.vector.memset(win[:].bitcast(I32), 0)
        nc.vector.memset(ms[:].bitcast(I32), 0)
        nc.vector.memset(dealt[:], 0.0)

        def load_rows(v, src):
            nc.gpsimd.dma_start(out=rows[v:NP:32], in_=src.rearrange("(b g n) -> g b n", b=2, g=4))

        for q in range(4):
            nc.scalar.dma_start(
                out=stage[32 * q : 32 * q + 12, :],
                in_=tab_scales[:, 4 * q : 4 * q + 4, :].bitcast(I32),
            )
        warm = sb.tile([NP, 1], F32, name="warm")
        nc.scalar.activation(warm[:], dealt[:, 0:1], ACT.Silu)
        nc.sync.dma_start(offs_t[:], offs)
        load_tab(0)
        for q in range(4):
            nc.sync.dma_start(
                out=wsr[32 * q : 32 * q + 4, :, :].bitcast(I32),
                in_=w4_scales[:, 4 * q : 4 * q + 4, :].rearrange("a r n -> r a n").bitcast(I32),
            )
        nc.sync.dma_start(out=w4r[:], in_=w4_words.rearrange("a p n -> p a n").bitcast(I32))
        load_w1(0)
        load_tab(1)
        nc.sync.dma_start(pos2_t[:], pos2)
        nc.sync.dma_start(pos1_t[:], pos1)
        for v, src in enumerate((gain, shift, focus)):
            load_rows(v, src)

        for q in range(4):
            live = slice(32 * q, 32 * q + 12)
            nc.vector.tensor_copy(out=win[:].bitcast(I32)[live], in_=stage[live])
        gs = sb.tile([NP, S], U8, name="gs", align_bytes=64)
        nc.vector.tensor_copy(gs[:], win[:].indirect(offs_t[:]))
        nc.sync.dma_start(out=ms[0:112, :].bitcast(I32), in_=gs[4:116, :].bitcast(I32))
        load_tab(2)
        gw = [sb.tile([NP, S], U32, name="gw%d" % a, tag=("gw0", "gw1")[a], align_bytes=64) for a in range(2)]
        gw2 = [sb.tile([NP, 512], U32, name="gw2%d" % h, align_bytes=64) for h in range(2)]
        nc.vector.tensor_copy(gw[0][:], tab[0][:].bitcast(U32).indirect(offs_t[:]))

        w4p = sb.tile([NP, 2, 8, 256], U8, name="w4p", align_bytes=64)
        wsp = sb.tile([NP, 2, 8, 128], U8, name="wsp", align_bytes=64)
        nc.vector.tensor_copy(
            out=w4p[:].rearrange("p a c n -> p (a c n)").bitcast(I32).rearrange("p (g t q w) -> p g t q w", g=4, t=4, w=4),
            in_=w4r[:].rearrange("p a (b q t w) -> p (a b) t q w", b=2, t=4, w=4),
        )
        wsp_words = wsp[:].rearrange("p a c n -> p (a c n)").bitcast(I32)
        wsr_words = wsr[:].rearrange("p a n -> p (a n)").bitcast(I32)
        nc.vector.memset(wsp_words, 0)
        for q in range(4):
            live = slice(32 * q, 32 * q + 4)
            nc.vector.tensor_copy(
                out=wsp_words[live].rearrange("p (g t q w) -> p g t q w", g=4, t=4, w=2),
                in_=wsr_words[live].rearrange("p (g q t w) -> p g t q w", g=4, t=4, w=2),
            )

        w1b = [sb.tile([NP, 2048], BF16, name="w1b%d" % b, tag=("w1b", "win")[b], align_bytes=64) for b in range(2)]
        w1c = [sb.tile([NP, 512], U32, name="w1c%d" % b, align_bytes=64) for b in range(2)]
        w1s = [sb.tile([NP, 512], U8, name="w1s%d" % b, align_bytes=64) for b in range(2)]

        def round_w1(b, copy):
            copy(
                out=w1b[b][:].rearrange("p (t q i j) -> p t q i j", t=4, i=8, j=4),
                in_=w1r[b][:].rearrange("p j (q t i) -> p t q i j", t=4, i=8),
            )
            nc.vector.quantize_mx(out=w1c[b][:].bitcast(FP8X4), scales=w1s[b][:], in_=w1b[b][:])

        round_w1(0, nc.scalar.copy)
        load_w1(1)
        nc.vector.tensor_copy(gw[1][:], tab[1][:].bitcast(U32).indirect(offs_t[:]))
        nc.sync.dma_start(out=sway_t[:], in_=sway.partition_broadcast(NP))
        for g in range(4):
            live = slice(32 * g, 32 * g + 3)
            nc.vector.tensor_copy(
                out=dealt[live].rearrange("p (b t r i) -> p b t r i", b=2, t=4, i=8),
                in_=rows[live].rearrange("p b (r t i) -> p b t r i", t=4, i=8),
            )
        nc.vector.transpose(turned[:].rearrange("p c v -> p (c v)"), dealt[:])
        sgn = sb.tile([NP, 8], F32, name="sgn")
        fac = [sb.tile([NP, 8], F32, name="fac%d" % v) for v in range(4)]
        nc.vector.tensor_scalar(sgn[:], turned[:, :, 2], 0.0, 2.0, ALU.is_ge, ALU.mult)
        for v in range(2):
            nc.vector.scalar_tensor_tensor(fac[v][:], sgn[:], -1.0, turned[:, :, v], ALU.add, ALU.mult)
            nc.vector.tensor_tensor(fac[2 + v][:], turned[:, :, v], turned[:, :, 2], ALU.mult)

        for h in range(2):
            nc.vector.tensor_copy(gw2[h][:], tab[2][:].bitcast(U32).indirect(offs_t[:, 32 * h : 32 * (h + 1)]))
        round_w1(1, nc.vector.tensor_copy)

        tanh_t = [sb.tile([NP, S], F32, name="tanh%d" % c) for c in range(8)]

        def first_pass(acc, c, h, a):
            cols = slice(512 * h, 512 * (h + 1))
            if a < 2:
                nc.tensor.matmul_mx(
                    out=acc[:],
                    lhsT=w4p[:, a, c, :].bitcast(FP4X4),
                    lhsT_scale=wsp[:, a, c, :],
                    rhs=gw[a][:, cols].bitcast(FP8X4),
                    rhs_scale=(gs, ms)[a][:, cols],
                    start=(a == 0),
                    stop=False,
                )
            else:
                b, t = divmod(c, 4)
                wc = slice(128 * t, 128 * (t + 1))
                nc.tensor.matmul_mx(
                    out=acc[:],
                    lhsT=w1c[b][:, wc].bitcast(FP8X4),
                    lhsT_scale=w1s[b][:, wc],
                    rhs=gw2[h][:].bitcast(FP8X4),
                    rhs_scale=gs[8:NP, cols],
                    start=False,
                    stop=True,
                )
                nc.scalar.activation(tanh_t[c][:, cols], acc[:], ACT.Tanh)

        early = [[ps.tile([NP, 512], F32, name="acc%d_%d" % (c, h), tag="bank%d" % (2 * c + h)) for h in range(2)] for c in range(4)]
        for a in range(3):
            for c in range(4):
                for h in range(2):
                    first_pass(early[c][h], c, h, a)
        for c in range(4, 8):
            for h in range(2):
                acc = ps.tile([NP, 512], F32, name="acc%d_%d" % (c, h), tag="bank%d" % (2 * (c % 2) + h))
                for a in range(3):
                    first_pass(acc, c, h, a)

        ring = sb.tile([NP, 5 * P], F32, name="ring")
        picked1 = [sb.tile([NP, P], F32, name="picked1_%d" % c) for c in range(3)]
        pl2 = [sb.tile([NP, 4, P], BF16, name="pl2_%d" % b) for b in range(2)]
        pl1 = [sb.tile([NP, 4, P], BF16, name="pl1_%d" % b) for b in range(2)]
        il2 = [sb.tile([NP, P, 4], BF16, name="il2_%d" % b, align_bytes=64) for b in range(2)]
        il1 = [[sb.tile([NP, HALF, 4], BF16, name="il1_%d_%d" % (u, b), align_bytes=64) for b in range(2)] for u in range(2)]
        c2 = [sb.tile([NP, P], U32, name="c2_%d" % b, align_bytes=64) for b in range(2)]
        s2 = [sb.tile([NP, P], U8, name="s2_%d" % b, align_bytes=64) for b in range(2)]
        c1 = [[sb.tile([NP, HALF], U32, name="c1_%d_%d" % (u, b), align_bytes=64) for b in range(2)] for u in range(2)]
        s1 = [[sb.tile([NP, HALF], U8, name="s1_%d_%d" % (u, b), align_bytes=64) for b in range(2)] for u in range(2)]
        e_ps = [ps.tile([NP, P], F32, name="e%d" % m, tag="bank%d" % (4 + m)) for m in range(4)]

        def pick2(c, at):
            b, t = divmod(c, 4)
            g = ring[:, at : at + P]
            nc.vector.tensor_copy(g, tanh_t[c][:].indirect(pos2_t[:]))
            nc.scalar.activation(pl2[b][:, t, :], g, ACT.Abs, bias=fac[3][:, c : c + 1], scale=fac[2][:, c : c + 1])

        def pick1(c):
            b, t = divmod(c, 4)
            g = picked1[c % 3][:]
            nc.vector.tensor_copy(g, tanh_t[c][:].indirect(pos1_t[:]))
            nc.gpsimd.tensor_scalar(pl1[b][:, t, :], g, fac[0][:, c : c + 1], fac[1][:, c : c + 1], ALU.mult, ALU.add)

        def weave(copy, dst, src, codes, scales):
            copy(
                out=dst[:].rearrange("p (c i) t -> p c t i", i=4),
                in_=src.rearrange("p t (c i) -> p c t i", i=4),
            )
            nc.vector.quantize_mx(out=codes[:].bitcast(FP8X4), scales=scales[:], in_=dst[:].rearrange("p n t -> p (n t)"))

        def second_pass(u, b):
            for mm in range(2):
                mc = slice(128 * mm, 128 * (mm + 1))
                nc.tensor.matmul_mx(
                    out=e_ps[2 * u + mm][:],
                    lhsT=c1[u][b][:, mc].bitcast(FP8X4),
                    lhsT_scale=s1[u][b][:, mc],
                    rhs=c2[b][:].bitcast(FP8X4),
                    rhs_scale=s2[b][:],
                    start=(b == 0),
                    stop=(b == 1),
                )

        def finish(m):
            turns = ep.tile([NP, P], I32, name="turns")
            frac = ep.tile([NP, P], F32, name="frac")
            wave = ep.tile([NP, P], F32, name="wave")
            res = sb.tile([NP, P], F32, name="res%d" % m)
            nc.vector.tensor_scalar(turns[:], e_ps[m][:], 1.0 / (2.0 * math.pi), None, ALU.mult)
            nc.vector.scalar_tensor_tensor(frac[:], e_ps[m][:], 1.0 / (2.0 * math.pi), turns[:], ALU.mult, ALU.subtract)
            nc.scalar.activation(wave[:], frac[:], ACT.Sin, scale=2.0 * math.pi)
            (nc.gpsimd, nc.vector)[m // 3].tensor_tensor(frac[:], wave[:], sway_t[:], ALU.mult)
            nc.vector.tensor_tensor(res[:], e_ps[m][:], frac[:], ALU.add)
            nc.sync.dma_start(out=out[128 * m : 128 * (m + 1), :], in_=res[:])

        for c in range(8):
            pick2(c, P * (c % 5))
            pick1(c)
            if c % 4 == 3:
                b = c // 4
                weave((nc.scalar.copy, nc.vector.tensor_copy)[b], il2[b], pl2[b][:], c2[b], s2[b])
                for u in range(2):
                    weave(nc.scalar.copy, il1[u][b], pl1[b][:, :, HALF * u : HALF * (u + 1)], c1[u][b], s1[u][b])
                    second_pass(u, b)
        for m in range(4):
            finish(m)
